import numpy as np
import ml_dtypes


def mxq(x, axis, fmt="e4m3"):
    dtype, down = {"e4m3": (ml_dtypes.float8_e4m3fn, 7), "e5m2": (ml_dtypes.float8_e5m2, 14)}[fmt]
    v = np.moveaxis(np.asarray(x, np.float32).astype(ml_dtypes.bfloat16).astype(np.float64), axis, -1)
    blocks = v.reshape(v.shape[:-1] + (-1, 32))
    amax = np.abs(blocks).max(-1, keepdims=True)
    byte = np.maximum(np.where(amax > 0, np.frexp(amax)[1] - 1 + 127, 0) - down, 1)
    scale = np.exp2(byte - 127.0)
    codes = (blocks / scale).astype(np.float32).astype(dtype).astype(np.float64)
    return np.moveaxis((codes * scale).reshape(v.shape), -1, axis)


WIDE = False


def mx_kscale(k):
    if not WIDE:
        return np.ones(k)
    levels = np.array([10, -10, 5, -5, 0])
    if k % 512:
        return np.exp2(np.random.permutation(np.resize(levels, k // 32))).repeat(32)
    a = np.empty((k // 512, 16))
    for p in range(k // 512):
        a[p, :8] = np.random.permutation(np.resize(levels, 8))
        for g in range(8):
            far = levels[np.abs(levels - a[p, g]) >= 10]
            a[p, g + 8] = far[np.random.randint(len(far))]
    return np.exp2(a.ravel()).repeat(32)


def f64(x):
    return np.asarray(x).astype(np.float64)


def striped(idx):
    return np.tile(idx.reshape(-1, 16).T, (8, 1)).astype(np.uint16)


def unstriped(offs):
    return offs[:16].T.reshape(-1).astype(np.int64)


def pack_weight(w):
    k, n = w.shape
    w = f64(np.asarray(w, np.float32).astype(ml_dtypes.bfloat16)).reshape(k // 32, 32, n)
    amax = np.abs(w).max(1)
    byte = np.clip(np.where(amax > 0, np.frexp(amax)[1] - 1 + 127 - 7, 1), 1, 254)
    scaled = (w * np.exp2(127.0 - byte)[:, None, :]).reshape(k, n).astype(np.float32)
    words = np.ascontiguousarray(scaled.reshape(k // 512, 128, 4, n).transpose(0, 1, 3, 2)).astype(ml_dtypes.float8_e4m3fn).view(np.uint8)
    return words, np.ascontiguousarray(byte.astype(np.uint8).reshape(k // 512, 16, n))


def unpack_weight(words, scales):
    g, p, n, _ = words.shape
    vals = np.ascontiguousarray(words).view(ml_dtypes.float8_e4m3fn).astype(np.float64) * np.repeat(np.exp2(scales.astype(np.float64) - 127.0), 8, axis=1)[..., None]
    return vals.transpose(0, 1, 3, 2).reshape(g * 512, n)


K, T, S, D, H, Z, W = 512, 2048, 512, 2, 512, 512, 2048
P = 2 ** 7


def setup_inputs():
    n = np.random.standard_normal
    s = mx_kscale(K)[:, None]
    packed_xT = pack_weight(n((K, T)) * s)
    packed_eT = pack_weight(n((K, W)) * s)
    return {
        "x_words": packed_xT[0],
        "x_scales": packed_xT[1],
        "w1": (n((K, H)) / np.sqrt(K) / s).astype(np.float32),
        "e_words": packed_eT[0],
        "e_scales": packed_eT[1],
        "unit": (np.random.uniform(0.6, 1.4, (K, 1)) / np.sqrt(K) / s).astype(np.float32),
        "len_": (np.tile(np.random.uniform(0.4, 1.6, W), (P, 1))).astype(np.float32),
        "offs": striped(np.random.permutation(T)[:S]),
        "nxt": striped(np.random.permutation(S)),
        "road": striped(np.random.permutation(W)[:Z]),
        "con": striped(np.random.permutation(Z)),
    }


def reference(x_words, x_scales, w1, e_words, e_scales, unit, len_, offs, nxt, road, con):
    xq = unpack_weight(x_words, x_scales)[:, unstriped(offs)]
    y = mxq(f64(w1), 0, "e4m3").T @ xq
    yn = y[:, unstriped(nxt)]
    vel = yn - y
    vy = vel * np.abs(y)
    traj = vy.reshape(len(vy), -1, D).sum(axis=2)
    tn = traj / (np.abs(traj) + 0.8)
    hid = f64(unit) * tn
    e_road = unpack_weight(e_words, e_scales)[:, unstriped(road)]
    sc = mxq(hid, 0, "e4m3").T @ e_road
    ds = sc - (f64(len_)[:1][:, unstriped(road)])
    emis = -1.0 * ((ds) ** 2)
    prevm = emis[:, unstriped(con)]
    path = prevm - (0.8 * (f64(len_)[:1][:, unstriped(road)]))
    return np.maximum(emis, path)

@@ -1,0 +1,293 @@
+from contextlib import ExitStack
+
+import concourse.mybir as mybir
+
+F32 = mybir.dt.float32
+BF16 = mybir.dt.bfloat16
+I32 = mybir.dt.int32
+U32 = mybir.dt.uint32
+U16 = mybir.dt.uint16
+U8 = mybir.dt.uint8
+FP8X4 = mybir.dt.float8_e4m3fn_x4
+ALU = mybir.AluOpType
+ACT = mybir.ActivationFunctionType
+
+P = 128
+PACK = 4
+K = 512
+TABLE = 2048
+S = 512
+HALF = S // 2
+V = 256
+SAT = 0.8
+PEN = 0.8
+CAST_SPLIT = 80
+DIRECT = (0,1,2,3)
+Y_ON_SCALAR = (1,)
+MAG_ON_VECTOR = ()
+FETCH_ON_SCALAR = ((0,0),(0,1),(1,0),(1,1),(2,0),(2,1),(3,0),(3,1),)
+
+FLOPS = 2 * K * K * S + 2 * K * V * S
+
+
+def tile_picked_ytrajcl_max_p_kernel(
+    tc, x_words, x_scales, w1, e_words, e_scales, unit, len_, offs, nxt, road, con, out
+):
+    nc = tc.nc
+    with ExitStack() as ctx:
+        keep = ctx.enter_context(tc.tile_pool(name="keep", bufs=1))
+        psum = ctx.enter_context(tc.psum_pool(name="psum", bufs=8))
+
+        def sb(name, shape, dtype, tag=None):
+            return keep.tile(shape, dtype, name=name, tag=tag or name, align_bytes=64)
+
+        def bank(tag, shape):
+            return psum.tile(shape, F32, name=tag, tag="bank")
+
+        def half_of(lst, h):
+            return lst[:, h * (HALF // 16) : (h + 1) * (HALF // 16)]
+
+        offs_sb = sb("offs_sb", [P, S // 16], U16)
+        nxt_sb = sb("nxt_sb", [P, S // 16], U16)
+        road_sb = sb("road_sb", [P, S // 16], U16)
+        con_sb = sb("con_sb", [P, S // 16], U16)
+        w_raw = sb("w_raw", [P, PACK, K], F32)
+        x_table = sb("x_table", [P, TABLE], U32)
+        e_table = sb("e_table", [P, TABLE], U32)
+        xs_table = sb("xs_table", [P, TABLE], U8)
+        es_table = sb("es_table", [P, TABLE], U8)
+        len_cols = sb("len_cols", [P, TABLE // P], F32)
+        len_table = sb("len_table", [P, TABLE], F32)
+        unit_sb = sb("unit_sb", [P, PACK], F32)
+        ident = sb("ident", [P, P], F32)
+
+        nc.gpsimd.memset(xs_table[:].bitcast(I32), 0)
+        nc.gpsimd.memset(es_table[:].bitcast(I32), 0)
+        ones = sb("ones", [P, P], F32)
+        ramp = sb("ramp", [P, P], F32)
+        base = sb("base", [P, 1], F32)
+        within = sb("within", [P, 32], F32)
+        row = sb("row", [P, 1], F32)
+        nc.vector.memset(ones[:], 1.0)
+        for q in range(4):
+            nc.vector.memset(base[32 * q : 32 * q + 32, :], 32.0 * q)
+        nc.vector.tensor_tensor_scan(ramp[:], ones[:], ones[:], 0.0, ALU.mult, ALU.add)
+        nc.vector.transpose(within[:], ramp[:, 0:32])
+        nc.vector.tensor_tensor(row[:], within[:, 0:1], base[:], ALU.add)
+        nc.vector.tensor_scalar(ident[:], ramp[:], row[:], None, ALU.is_equal)
+        nc.sync.dma_start(offs_sb[:], offs)
+        nc.scalar.dma_start(out=len_cols[:], in_=len_[0].rearrange("(p c) -> p c", p=P))
+        nc.sync.dma_start(out=w_raw[:], in_=w1.rearrange("(p j) c -> p j c", j=PACK))
+        for q in range(4):
+            nc.sync.dma_start(
+                out=xs_table[32 * q : 32 * q + 4, :].bitcast(I32), in_=x_scales[0, 4 * q : 4 * q + 4, :].bitcast(I32)
+            )
+        nc.sync.dma_start(out=x_table[:].bitcast(I32), in_=x_words[0].rearrange("p n t -> p (n t)").bitcast(I32))
+        nc.sync.dma_start(road_sb[:], road)
+        for q in range(4):
+            nc.sync.dma_start(
+                out=es_table[32 * q : 32 * q + 4, :].bitcast(I32), in_=e_scales[0, 4 * q : 4 * q + 4, :].bitcast(I32)
+            )
+        nc.sync.dma_start(nxt_sb[:], nxt)
+        nc.sync.dma_start(out=e_table[:].bitcast(I32), in_=e_words[0].rearrange("p n t -> p (n t)").bitcast(I32))
+        nc.sync.dma_start(out=unit_sb[:], in_=unit.rearrange("(p t) o -> p (t o)", t=PACK))
+        nc.sync.dma_start(con_sb[:], con)
+
+        len_view = len_table[:].rearrange("p (n c) -> p n c", c=TABLE // P)
+        for b in range(4):
+            spread = bank("spread", [P, 4, P])
+            for c in range(4):
+                col = 4 * b + c
+                nc.tensor.transpose(spread[:, c, :], len_cols[:, col : col + 1].to_broadcast([P, P]), ident[:])
+            dst = len_view[:, :, 4 * b : 4 * b + 4]
+            src = spread[:].rearrange("p c n -> p n c")
+            if b >= 2:
+                nc.scalar.copy(dst, src)
+            else:
+                nc.vector.tensor_copy(dst, src)
+
+        w_bf = sb("w_bf", [P, PACK, P, PACK], BF16)
+        w_src = w_raw[:].rearrange("p j (m t) -> p m j t", t=PACK)
+        w_dst = w_bf[:].rearrange("p t m j -> p m j t")
+        nc.scalar.copy(w_dst[:, :CAST_SPLIT], w_src[:, :CAST_SPLIT])
+        nc.vector.tensor_copy(w_dst[:, CAST_SPLIT:], w_src[:, CAST_SPLIT:])
+        xs = sb("xs", [P, S], U8)
+        nc.vector.tensor_copy(xs[:], xs_table[:].indirect(offs_sb[:]))
+        wq = sb("wq", [P, K], U32)
+        ws = sb("ws", [P, K], U8)
+        nc.vector.quantize_mx(out=wq[:].bitcast(FP8X4), scales=ws[:], in_=w_bf[:].rearrange("p t m j -> p (t m j)"))
+
+        length = sb("length", [P, S], F32)
+        penalty = sb("penalty", [P, S], F32)
+        nc.scalar.activation(length[:], len_table[:].indirect(road_sb[:]), ACT.Copy)
+        nc.scalar.activation(penalty[:], length[:], ACT.Copy, scale=-PEN)
+
+        xq = [sb("xq%d" % h, [P, HALF], U32) for h in range(2)]
+        y_ps = [bank("y_ps", [P, S]) for t in range(PACK)]
+        for h in range(2):
+            nc.vector.tensor_copy(xq[h][:], x_table[:].indirect(half_of(offs_sb, h)))
+        for pair in range(2):
+            for h in range(2):
+                cols = slice(h * HALF, (h + 1) * HALF)
+                for t in (2 * pair, 2 * pair + 1):
+                    nc.tensor.matmul_mx(
+                        out=y_ps[t][:, cols],
+                        lhsT=wq[:, t * P : (t + 1) * P].bitcast(FP8X4),
+                        lhsT_scale=ws[:, t * P : (t + 1) * P],
+                        rhs=xq[h][:].bitcast(FP8X4),
+                        rhs_scale=xs[:, cols],
+                        start=True,
+                        stop=True,
+                    )
+        es = sb("es", [P, S], U8)
+        nc.vector.tensor_copy(es[:], es_table[:].indirect(road_sb[:]))
+
+        y = [sb("y%d" % t, [P, S], F32) for t in range(PACK)]
+        mag = [sb("mag%d" % t, [P, S], F32) for t in range(PACK)]
+        traj = {}
+
+        def members(tile, h, d):
+            return tile[:, h * HALF + d : (h + 1) * HALF : 2]
+
+        def window(t):
+            if t in Y_ON_SCALAR:
+                nc.scalar.copy(y[t][:], y_ps[t][:])
+            else:
+                nc.vector.tensor_copy(y[t][:], y_ps[t][:])
+
+        def magnitude(t):
+            if t in MAG_ON_VECTOR:
+                nc.vector.scalar_tensor_tensor(mag[t][:], y[t][:], -1.0, y[t][:], ALU.mult, ALU.max)
+            elif t in DIRECT:
+                nc.scalar.activation(mag[t][:], y[t][:], ACT.Abs)
+            else:
+                turned = bank("turned", [P, 4, P])
+                for h in range(2):
+                    for d in range(2):
+                        nc.tensor.transpose(turned[:, 2 * h + d, :], members(y[t], h, d), ident[:])
+                nc.scalar.activation(mag[t][:], turned[:].rearrange("p b m -> p (b m)"), ACT.Abs)
+
+        yn = {}
+        traj = [sb("traj%d" % h, [P, PACK, P], F32) for h in range(2)]
+        size = [sb("size%d" % h, [P, PACK, P], F32) for h in range(2)]
+        root = [sb("root%d" % h, [P, PACK, P], F32) for h in range(2)]
+        part = [sb("part%d" % h, [P, PACK, P], F32) for h in range(2)]
+
+        def fetch(t, h):
+            yn[t, h] = sb("yn%d%d" % (t, h), [P, HALF], F32)
+            src = y[t][:].indirect(half_of(nxt_sb, h))
+            if (t, h) in FETCH_ON_SCALAR:
+                nc.scalar.activation(yn[t, h][:], src, ACT.Copy)
+            else:
+                nc.vector.tensor_copy(yn[t, h][:], src)
+
+        def combine(t, h):
+            cols = slice(h * HALF, (h + 1) * HALF)
+            vel = sb("vel%d%d" % (t, h), [P, HALF], F32)
+            vy = sb("vy%d%d" % (t, h), [P, HALF], F32)
+            nc.vector.tensor_tensor(vel[:], yn[t, h][:], y[t][:, cols], ALU.subtract)
+            nc.vector.tensor_tensor(vy[:], vel[:], mag[t][:, cols], ALU.mult)
+            nc.vector.tensor_tensor(traj[h][:, t, :], vy[:, 0::2], vy[:, 1::2], ALU.add)
+
+        def step(t, h):
+            fetch(t, h)
+            combine(t, h)
+
+        def saturate(h, t0, t1):
+            nc.scalar.activation(size[h][:, t0:t1, :], traj[h][:, t0:t1, :], ACT.Abs)
+            nc.scalar.activation(root[h][:, t0:t1, :], size[h][:, t0:t1, :], ACT.Abs_reciprocal_sqrt, bias=SAT)
+            for t in range(t0, t1):
+                nc.vector.scalar_tensor_tensor(
+                    part[h][:, t, :], traj[h][:, t, :], unit_sb[:, t : t + 1], root[h][:, t, :], ALU.mult, ALU.mult
+                )
+
+        eq = sb("eq", [P, S], U32)
+
+        def scores(h):
+            hid = sb("hid%d" % h, [P, P, PACK], BF16)
+            nc.vector.tensor_tensor(
+                hid[:].rearrange("p (b i) t -> p b t i", i=4),
+                part[h][:].rearrange("p t (b i) -> p b t i", i=4),
+                root[h][:].rearrange("p t (b i) -> p b t i", i=4),
+                ALU.mult,
+            )
+            hq = sb("hq%d" % h, [P, P], U32)
+            hs = sb("hs%d" % h, [P, P], U8)
+            nc.vector.quantize_mx(out=hq[:].bitcast(FP8X4), scales=hs[:], in_=hid[:].rearrange("p v t -> p (v t)"))
+            sc = bank("sc", [P, S])
+            nc.tensor.matmul_mx(
+                out=sc[:],
+                lhsT=hq[:].bitcast(FP8X4),
+                lhsT_scale=hs[:],
+                rhs=eq[:].bitcast(FP8X4),
+                rhs_scale=es[:],
+                start=True,
+                stop=True,
+            )
+            return sc
+
+        def squares(sc, h):
+            ds = sb("ds%d" % h, [P, S], F32)
+            nc.vector.tensor_tensor(ds[:], sc[:], length[:], ALU.subtract)
+            sq = sb("sq%d" % h, [P, S], F32)
+            nc.scalar.activation(sq[:], ds[:], ACT.Square)
+            return sq
+
+        def emit(sq, h, g):
+            cols = slice(g * HALF, (g + 1) * HALF)
+            prev = sb("prev%d%d" % (h, g), [P, HALF], F32)
+            nc.scalar.activation(prev[:], sq[:].indirect(half_of(con_sb, g)), ACT.Copy, scale=-1.0)
+            path = sb("path%d%d" % (h, g), [P, HALF], F32)
+            nc.vector.tensor_tensor(path[:], prev[:], penalty[:, cols], ALU.add)
+            best = sb("best%d%d" % (h, g), [P, HALF], F32)
+            nc.vector.scalar_tensor_tensor(best[:], sq[:, cols], -1.0, path[:], ALU.mult, ALU.max)
+            nc.sync.dma_start(out=out[h * P : (h + 1) * P, cols], in_=best[:])
+
+        def emit1(sc1):
+            lo, hi = slice(0, HALF), slice(HALF, S)
+            ds_lo = sb("ds_lo", [P, HALF], F32)
+            ds_hi = sb("ds_hi", [P, HALF], F32)
+            sq_lo = sb("sq_lo", [P, HALF], F32)
+            emis = sb("emis", [P, S], F32)
+            nc.vector.tensor_tensor(ds_lo[:], sc1[:, lo], length[:, lo], ALU.subtract)
+            nc.vector.tensor_tensor(ds_hi[:], sc1[:, hi], length[:, hi], ALU.subtract)
+            nc.scalar.activation(sq_lo[:], ds_lo[:], ACT.Square)
+            nc.scalar.activation(emis[:, lo], sq_lo[:], ACT.Copy, scale=-1.0)
+            nc.vector.scalar_tensor_tensor(emis[:, hi], ds_hi[:], -1.0, ds_hi[:], ALU.mult, ALU.mult)
+            path_lo = sb("path_lo", [P, HALF], F32)
+            nc.vector.tensor_tensor(path_lo[:], emis[:].indirect(half_of(con_sb, 0)), penalty[:, lo], ALU.add)
+            prev_hi = sb("prev_hi", [P, HALF], F32)
+            nc.scalar.activation(prev_hi[:], emis[:].indirect(half_of(con_sb, 1)), ACT.Copy)
+            best_lo = sb("best_lo", [P, HALF], F32)
+            nc.vector.tensor_tensor(best_lo[:], path_lo[:], emis[:, lo], ALU.max)
+            nc.sync.dma_start(out=out[P:V, lo], in_=best_lo[:])
+            path_hi = sb("path_hi", [P, HALF], F32)
+            nc.vector.tensor_tensor(path_hi[:], prev_hi[:], penalty[:, hi], ALU.add)
+            best_hi = sb("best_hi", [P, HALF], F32)
+            nc.vector.tensor_tensor(best_hi[:], path_hi[:], emis[:, hi], ALU.max)
+            nc.sync.dma_start(out=out[P:V, hi], in_=best_hi[:])
+
+        def gather_e_scales():
+            nc.vector.tensor_copy(es[:], es_table[:].indirect(road_sb[:]))
+
+        def gather_e_words():
+            nc.vector.tensor_copy(eq[:], e_table[:].indirect(road_sb[:]))
+
+        for t in range(PACK):
+            window(t)
+            fetch(t, 0)
+            magnitude(t)
+            combine(t, 0)
+        gather_e_words()
+        saturate(0, 0, 2)
+        saturate(0, 2, 4)
+        sc0 = scores(0)
+        for t in range(PACK):
+            step(t, 1)
+        sq0 = squares(sc0, 0)
+        saturate(1, 0, 2)
+        saturate(1, 2, 4)
+        sc1 = scores(1)
+        emit(sq0, 0, 0)
+        emit(sq0, 0, 1)
+        emit1(sc1)

@@ -13,19 +13,22 @@ ALU = mybir.AluOpType
 ACT = mybir.ActivationFunctionType
 
 P = 128
+QUAD = 32
 PACK = 4
 K = 512
 TABLE = 2048
 S = 512
 HALF = S // 2
 V = 256
-SAT = 0.8
-PEN = 0.8
-CAST_SPLIT = 80
-DIRECT = (0,1,2,3)
-Y_ON_SCALAR = (1,)
-MAG_ON_VECTOR = ()
-FETCH_ON_SCALAR = ((0,0),(0,1),(1,0),(1,1),(2,0),(2,1),(3,0),(3,1),)
+GROUP = 16
+PSUM_BANKS = 8
+SATURATION = 0.8
+PENALTY = 0.8
+FLOAT_BIG = 3.0e38
+
+CAST_ON_SCALAR = 64
+COPY_ON_SCALAR = (1,)
+FETCH_ON_VECTOR = ((2, 0), (3, 0))
 
 FLOPS = 2 * K * K * S + 2 * K * V * S
 
@@ -36,187 +39,193 @@ def tile_picked_ytrajcl_max_p_kernel(
     nc = tc.nc
     with ExitStack() as ctx:
         keep = ctx.enter_context(tc.tile_pool(name="keep", bufs=1))
-        psum = ctx.enter_context(tc.psum_pool(name="psum", bufs=8))
+        psum = ctx.enter_context(tc.psum_pool(name="psum", bufs=PSUM_BANKS))
 
         def sb(name, shape, dtype, tag=None):
             return keep.tile(shape, dtype, name=name, tag=tag or name, align_bytes=64)
 
-        def bank(tag, shape):
-            return psum.tile(shape, F32, name=tag, tag="bank")
+        def bank(name, shape):
+            return psum.tile(shape, F32, name=name, tag="bank")
 
-        def half_of(lst, h):
-            return lst[:, h * (HALF // 16) : (h + 1) * (HALF // 16)]
+        def half(n):
+            return slice(n * HALF, (n + 1) * HALF)
 
-        offs_sb = sb("offs_sb", [P, S // 16], U16)
-        nxt_sb = sb("nxt_sb", [P, S // 16], U16)
-        road_sb = sb("road_sb", [P, S // 16], U16)
-        con_sb = sb("con_sb", [P, S // 16], U16)
-        w_raw = sb("w_raw", [P, PACK, K], F32)
-        x_table = sb("x_table", [P, TABLE], U32)
+        def list_half(entries, n):
+            return entries[:, n * (HALF // GROUP) : (n + 1) * (HALF // GROUP)]
+
+        offs_sb = sb("offs_sb", [P, S // GROUP], U16)
+        nxt_sb = sb("nxt_sb", [P, S // GROUP], U16)
+        road_sb = sb("road_sb", [P, S // GROUP], U16)
+        con_sb = sb("con_sb", [P, S // GROUP], U16)
+        w_raw = sb("w_raw", [P, PACK, K], F32, tag="w_raw")
+        x_table = sb("x_table", [P, TABLE], U32, tag="x_table")
         e_table = sb("e_table", [P, TABLE], U32)
         xs_table = sb("xs_table", [P, TABLE], U8)
         es_table = sb("es_table", [P, TABLE], U8)
         len_cols = sb("len_cols", [P, TABLE // P], F32)
-        len_table = sb("len_table", [P, TABLE], F32)
         unit_sb = sb("unit_sb", [P, PACK], F32)
         ident = sb("ident", [P, P], F32)
 
         nc.gpsimd.memset(xs_table[:].bitcast(I32), 0)
         nc.gpsimd.memset(es_table[:].bitcast(I32), 0)
+
         ones = sb("ones", [P, P], F32)
         ramp = sb("ramp", [P, P], F32)
         base = sb("base", [P, 1], F32)
-        within = sb("within", [P, 32], F32)
+        within = sb("within", [P, QUAD], F32)
         row = sb("row", [P, 1], F32)
         nc.vector.memset(ones[:], 1.0)
-        for q in range(4):
-            nc.vector.memset(base[32 * q : 32 * q + 32, :], 32.0 * q)
+        for q in range(P // QUAD):
+            nc.vector.memset(base[QUAD * q : QUAD * (q + 1), :], float(QUAD * q))
         nc.vector.tensor_tensor_scan(ramp[:], ones[:], ones[:], 0.0, ALU.mult, ALU.add)
-        nc.vector.transpose(within[:], ramp[:, 0:32])
+        nc.vector.transpose(within[:], ramp[:, 0:QUAD])
         nc.vector.tensor_tensor(row[:], within[:, 0:1], base[:], ALU.add)
         nc.vector.tensor_scalar(ident[:], ramp[:], row[:], None, ALU.is_equal)
-        nc.sync.dma_start(offs_sb[:], offs)
-        nc.scalar.dma_start(out=len_cols[:], in_=len_[0].rearrange("(p c) -> p c", p=P))
-        nc.sync.dma_start(out=w_raw[:], in_=w1.rearrange("(p j) c -> p j c", j=PACK))
-        for q in range(4):
-            nc.sync.dma_start(
-                out=xs_table[32 * q : 32 * q + 4, :].bitcast(I32), in_=x_scales[0, 4 * q : 4 * q + 4, :].bitcast(I32)
-            )
-        nc.sync.dma_start(out=x_table[:].bitcast(I32), in_=x_words[0].rearrange("p n t -> p (n t)").bitcast(I32))
-        nc.sync.dma_start(road_sb[:], road)
-        for q in range(4):
-            nc.sync.dma_start(
-                out=es_table[32 * q : 32 * q + 4, :].bitcast(I32), in_=e_scales[0, 4 * q : 4 * q + 4, :].bitcast(I32)
-            )
-        nc.sync.dma_start(nxt_sb[:], nxt)
-        nc.sync.dma_start(out=e_table[:].bitcast(I32), in_=e_words[0].rearrange("p n t -> p (n t)").bitcast(I32))
+
+        def load_words(table, words):
+            nc.sync.dma_start(out=table[:].bitcast(I32), in_=words[0].rearrange("p n t -> p (n t)").bitcast(I32))
+
+        def load_scales(table, scales):
+            for r in range(PACK):
+                nc.sync.dma_start(
+                    out=table[r:P:QUAD, :].bitcast(I32), in_=scales[0, r : K // QUAD : PACK, :].bitcast(I32)
+                )
+
+        nc.sync.dma_start(out=len_cols[:], in_=len_[0].rearrange("(p c) -> p c", p=P))
         nc.sync.dma_start(out=unit_sb[:], in_=unit.rearrange("(p t) o -> p (t o)", t=PACK))
+        nc.sync.dma_start(offs_sb[:], offs)
+        nc.sync.dma_start(out=w_raw[:], in_=w1.rearrange("(p j) c -> p j c", j=PACK))
+        load_scales(xs_table, x_scales)
+        load_words(x_table, x_words)
+        nc.sync.dma_start(road_sb[:], road)
+        load_scales(es_table, e_scales)
+        load_words(e_table, e_words)
+        nc.sync.dma_start(nxt_sb[:], nxt)
         nc.sync.dma_start(con_sb[:], con)
 
-        len_view = len_table[:].rearrange("p (n c) -> p n c", c=TABLE // P)
-        for b in range(4):
-            spread = bank("spread", [P, 4, P])
-            for c in range(4):
-                col = 4 * b + c
-                nc.tensor.transpose(spread[:, c, :], len_cols[:, col : col + 1].to_broadcast([P, P]), ident[:])
-            dst = len_view[:, :, 4 * b : 4 * b + 4]
-            src = spread[:].rearrange("p c n -> p n c")
-            if b >= 2:
-                nc.scalar.copy(dst, src)
-            else:
-                nc.vector.tensor_copy(dst, src)
+        warm = sb("warm", [P, 1], F32)
+        warm_out = sb("warm_out", [P, 1], F32)
+        nc.vector.memset(warm[:], 1.0)
+        nc.scalar.activation(warm_out[:], warm[:], ACT.Abs_reciprocal_sqrt)
+
+        inverse = sb("inverse", [P, PACK], F32)
+        per_unit = sb("per_unit", [P, PACK], F32)
+        nc.vector.reciprocal(inverse[:], unit_sb[:])
+        nc.vector.tensor_scalar(per_unit[:], inverse[:], -FLOAT_BIG, FLOAT_BIG, ALU.max, ALU.min)
 
         w_bf = sb("w_bf", [P, PACK, P, PACK], BF16)
         w_src = w_raw[:].rearrange("p j (m t) -> p m j t", t=PACK)
         w_dst = w_bf[:].rearrange("p t m j -> p m j t")
-        nc.scalar.copy(w_dst[:, :CAST_SPLIT], w_src[:, :CAST_SPLIT])
-        nc.vector.tensor_copy(w_dst[:, CAST_SPLIT:], w_src[:, CAST_SPLIT:])
+        nc.scalar.copy(w_dst[:, :CAST_ON_SCALAR], w_src[:, :CAST_ON_SCALAR])
+        nc.vector.tensor_copy(w_dst[:, CAST_ON_SCALAR:], w_src[:, CAST_ON_SCALAR:])
         xs = sb("xs", [P, S], U8)
         nc.vector.tensor_copy(xs[:], xs_table[:].indirect(offs_sb[:]))
         wq = sb("wq", [P, K], U32)
         ws = sb("ws", [P, K], U8)
         nc.vector.quantize_mx(out=wq[:].bitcast(FP8X4), scales=ws[:], in_=w_bf[:].rearrange("p t m j -> p (t m j)"))
 
+        len_table = sb("len_table", [P, TABLE], F32, tag="w_raw")
+        len_view = len_table[:].rearrange("p (n c) -> p n c", c=TABLE // P)
+        per_bank = S // P
+        for first in range(0, TABLE // P, per_bank):
+            spread = bank("spread", [P, per_bank, P])
+            for c in range(per_bank):
+                column = len_cols[:, first + c : first + c + 1]
+                nc.tensor.transpose(spread[:, c, :], column.to_broadcast([P, P]), ident[:])
+            nc.scalar.copy(len_view[:, :, first : first + per_bank], spread[:].rearrange("p c n -> p n c"))
         length = sb("length", [P, S], F32)
-        penalty = sb("penalty", [P, S], F32)
         nc.scalar.activation(length[:], len_table[:].indirect(road_sb[:]), ACT.Copy)
-        nc.scalar.activation(penalty[:], length[:], ACT.Copy, scale=-PEN)
 
         xq = [sb("xq%d" % h, [P, HALF], U32) for h in range(2)]
         y_ps = [bank("y_ps", [P, S]) for t in range(PACK)]
         for h in range(2):
-            nc.vector.tensor_copy(xq[h][:], x_table[:].indirect(half_of(offs_sb, h)))
-        for pair in range(2):
+            nc.vector.tensor_copy(xq[h][:], x_table[:].indirect(list_half(offs_sb, h)))
+        for tiles in ((0, 1), (2, 3)):
             for h in range(2):
-                cols = slice(h * HALF, (h + 1) * HALF)
-                for t in (2 * pair, 2 * pair + 1):
+                for t in tiles:
                     nc.tensor.matmul_mx(
-                        out=y_ps[t][:, cols],
+                        out=y_ps[t][:, half(h)],
                         lhsT=wq[:, t * P : (t + 1) * P].bitcast(FP8X4),
                         lhsT_scale=ws[:, t * P : (t + 1) * P],
                         rhs=xq[h][:].bitcast(FP8X4),
-                        rhs_scale=xs[:, cols],
+                        rhs_scale=xs[:, half(h)],
                         start=True,
                         stop=True,
                     )
-        es = sb("es", [P, S], U8)
+        es = sb("es", [P, S], U8, tag="x_table")
         nc.vector.tensor_copy(es[:], es_table[:].indirect(road_sb[:]))
 
-        y = [sb("y%d" % t, [P, S], F32) for t in range(PACK)]
         mag = [sb("mag%d" % t, [P, S], F32) for t in range(PACK)]
-        traj = {}
+        scaled = [sb("scaled%d" % h, [P, PACK, P], F32) for h in range(2)]
+        size = [sb("size%d" % h, [P, PACK, P], F32) for h in range(2)]
+        root = [sb("root%d" % h, [P, PACK, P], F32) for h in range(2)]
+        damp = [sb("damp%d" % h, [P, PACK, P], F32) for h in range(2)]
 
-        def members(tile, h, d):
-            return tile[:, h * HALF + d : (h + 1) * HALF : 2]
-
-        def window(t):
-            if t in Y_ON_SCALAR:
+        y = []
+        for t in range(PACK):
+            y.append(sb("y%d" % t, [P, S], F32))
+            if t in COPY_ON_SCALAR:
                 nc.scalar.copy(y[t][:], y_ps[t][:])
             else:
                 nc.vector.tensor_copy(y[t][:], y_ps[t][:])
 
-        def magnitude(t):
-            if t in MAG_ON_VECTOR:
-                nc.vector.scalar_tensor_tensor(mag[t][:], y[t][:], -1.0, y[t][:], ALU.mult, ALU.max)
-            elif t in DIRECT:
-                nc.scalar.activation(mag[t][:], y[t][:], ACT.Abs)
-            else:
-                turned = bank("turned", [P, 4, P])
-                for h in range(2):
-                    for d in range(2):
-                        nc.tensor.transpose(turned[:, 2 * h + d, :], members(y[t], h, d), ident[:])
-                nc.scalar.activation(mag[t][:], turned[:].rearrange("p b m -> p (b m)"), ACT.Abs)
-
-        yn = {}
-        traj = [sb("traj%d" % h, [P, PACK, P], F32) for h in range(2)]
-        size = [sb("size%d" % h, [P, PACK, P], F32) for h in range(2)]
-        root = [sb("root%d" % h, [P, PACK, P], F32) for h in range(2)]
-        part = [sb("part%d" % h, [P, PACK, P], F32) for h in range(2)]
-
         def fetch(t, h):
-            yn[t, h] = sb("yn%d%d" % (t, h), [P, HALF], F32)
-            src = y[t][:].indirect(half_of(nxt_sb, h))
-            if (t, h) in FETCH_ON_SCALAR:
-                nc.scalar.activation(yn[t, h][:], src, ACT.Copy)
+            yn = sb("yn%d%d" % (t, h), [P, HALF], F32)
+            looked_up = y[t][:].indirect(list_half(nxt_sb, h))
+            if (t, h) in FETCH_ON_VECTOR:
+                nc.vector.tensor_copy(yn[:], looked_up)
             else:
-                nc.vector.tensor_copy(yn[t, h][:], src)
+                nc.scalar.activation(yn[:], looked_up, ACT.Copy)
+            return yn
 
-        def combine(t, h):
-            cols = slice(h * HALF, (h + 1) * HALF)
-            vel = sb("vel%d%d" % (t, h), [P, HALF], F32)
-            vy = sb("vy%d%d" % (t, h), [P, HALF], F32)
-            nc.vector.tensor_tensor(vel[:], yn[t, h][:], y[t][:, cols], ALU.subtract)
-            nc.vector.tensor_tensor(vy[:], vel[:], mag[t][:, cols], ALU.mult)
-            nc.vector.tensor_tensor(traj[h][:, t, :], vy[:, 0::2], vy[:, 1::2], ALU.add)
-
-        def step(t, h):
-            fetch(t, h)
-            combine(t, h)
-
-        def saturate(h, t0, t1):
-            nc.scalar.activation(size[h][:, t0:t1, :], traj[h][:, t0:t1, :], ACT.Abs)
-            nc.scalar.activation(root[h][:, t0:t1, :], size[h][:, t0:t1, :], ACT.Abs_reciprocal_sqrt, bias=SAT)
-            for t in range(t0, t1):
+        def trajectories(h, yn):
+            vel, vy = [], []
+            for t in range(PACK):
+                vel.append(sb("vel%d%d" % (t, h), [P, HALF], F32))
+                nc.vector.tensor_tensor(vel[t][:], yn[t][:], y[t][:, half(h)], ALU.subtract)
+            for t in range(PACK):
+                vy.append(sb("vy%d%d" % (t, h), [P, HALF], F32))
                 nc.vector.scalar_tensor_tensor(
-                    part[h][:, t, :], traj[h][:, t, :], unit_sb[:, t : t + 1], root[h][:, t, :], ALU.mult, ALU.mult
+                    vy[t][:], vel[t][:], unit_sb[:, t : t + 1], mag[t][:, half(h)], ALU.mult, ALU.mult
                 )
+            for t in range(PACK):
+                nc.vector.tensor_tensor(scaled[h][:, t, :], vy[t][:, 0::2], vy[t][:, 1::2], ALU.add)
 
-        eq = sb("eq", [P, S], U32)
+        yn0 = []
+        for t in range(PACK):
+            yn0.append(fetch(t, 0))
+            nc.scalar.activation(mag[t][:], y[t][:], ACT.Abs)
+        trajectories(0, yn0)
+        trajectories(1, [fetch(t, 1) for t in range(PACK)])
 
-        def scores(h):
+        eq = sb("eq", [P, S], U32, tag="vy31")
+        nc.vector.tensor_copy(eq[:], e_table[:].indirect(road_sb[:]))
+
+        for h in range(2):
+            for t in range(PACK):
+                nc.scalar.activation(size[h][:, t, :], scaled[h][:, t, :], ACT.Abs, scale=per_unit[:, t : t + 1])
+            for tiles in (slice(0, 2), slice(2, 4)):
+                nc.scalar.activation(
+                    root[h][:, tiles, :], size[h][:, tiles, :], ACT.Abs_reciprocal_sqrt, bias=SATURATION
+                )
+            for tiles in (slice(0, 2), slice(2, 4)):
+                nc.scalar.activation(damp[h][:, tiles, :], root[h][:, tiles, :], ACT.Square)
+
+        sc = []
+        for h in range(2):
             hid = sb("hid%d" % h, [P, P, PACK], BF16)
             nc.vector.tensor_tensor(
                 hid[:].rearrange("p (b i) t -> p b t i", i=4),
-                part[h][:].rearrange("p t (b i) -> p b t i", i=4),
-                root[h][:].rearrange("p t (b i) -> p b t i", i=4),
+                scaled[h][:].rearrange("p t (b i) -> p b t i", i=4),
+                damp[h][:].rearrange("p t (b i) -> p b t i", i=4),
                 ALU.mult,
             )
             hq = sb("hq%d" % h, [P, P], U32)
             hs = sb("hs%d" % h, [P, P], U8)
             nc.vector.quantize_mx(out=hq[:].bitcast(FP8X4), scales=hs[:], in_=hid[:].rearrange("p v t -> p (v t)"))
-            sc = bank("sc", [P, S])
+            sc.append(bank("sc", [P, S]))
             nc.tensor.matmul_mx(
-                out=sc[:],
+                out=sc[h][:],
                 lhsT=hq[:].bitcast(FP8X4),
                 lhsT_scale=hs[:],
                 rhs=eq[:].bitcast(FP8X4),
@@ -224,70 +233,39 @@ def tile_picked_ytrajcl_max_p_kernel(
                 start=True,
                 stop=True,
             )
-            return sc
 
-        def squares(sc, h):
-            ds = sb("ds%d" % h, [P, S], F32)
-            nc.vector.tensor_tensor(ds[:], sc[:], length[:], ALU.subtract)
-            sq = sb("sq%d" % h, [P, S], F32)
-            nc.scalar.activation(sq[:], ds[:], ACT.Square)
-            return sq
+        toll = sb("toll", [P, S], F32, tag="root1")
+        nc.scalar.activation(toll[:], length[:], ACT.Copy, scale=-PENALTY)
 
-        def emit(sq, h, g):
-            cols = slice(g * HALF, (g + 1) * HALF)
-            prev = sb("prev%d%d" % (h, g), [P, HALF], F32)
-            nc.scalar.activation(prev[:], sq[:].indirect(half_of(con_sb, g)), ACT.Copy, scale=-1.0)
-            path = sb("path%d%d" % (h, g), [P, HALF], F32)
-            nc.vector.tensor_tensor(path[:], prev[:], penalty[:, cols], ALU.add)
-            best = sb("best%d%d" % (h, g), [P, HALF], F32)
-            nc.vector.scalar_tensor_tensor(best[:], sq[:, cols], -1.0, path[:], ALU.mult, ALU.max)
-            nc.sync.dma_start(out=out[h * P : (h + 1) * P, cols], in_=best[:])
+        prev = {}
+        ds0 = sb("ds0", [P, S], F32, tag="hid1")
+        nc.vector.tensor_tensor(ds0[:], sc[0][:], length[:], ALU.subtract)
+        square = sb("square", [P, S], F32)
+        nc.scalar.activation(square[:], ds0[:], ACT.Square)
+        for g in range(2):
+            prev[0, g] = sb("prev0%d" % g, [P, HALF], F32)
+            nc.scalar.activation(prev[0, g][:], square[:].indirect(list_half(con_sb, g)), ACT.Copy, scale=-1.0)
 
-        def emit1(sc1):
-            lo, hi = slice(0, HALF), slice(HALF, S)
-            ds_lo = sb("ds_lo", [P, HALF], F32)
-            ds_hi = sb("ds_hi", [P, HALF], F32)
-            sq_lo = sb("sq_lo", [P, HALF], F32)
-            emis = sb("emis", [P, S], F32)
-            nc.vector.tensor_tensor(ds_lo[:], sc1[:, lo], length[:, lo], ALU.subtract)
-            nc.vector.tensor_tensor(ds_hi[:], sc1[:, hi], length[:, hi], ALU.subtract)
-            nc.scalar.activation(sq_lo[:], ds_lo[:], ACT.Square)
-            nc.scalar.activation(emis[:, lo], sq_lo[:], ACT.Copy, scale=-1.0)
-            nc.vector.scalar_tensor_tensor(emis[:, hi], ds_hi[:], -1.0, ds_hi[:], ALU.mult, ALU.mult)
-            path_lo = sb("path_lo", [P, HALF], F32)
-            nc.vector.tensor_tensor(path_lo[:], emis[:].indirect(half_of(con_sb, 0)), penalty[:, lo], ALU.add)
-            prev_hi = sb("prev_hi", [P, HALF], F32)
-            nc.scalar.activation(prev_hi[:], emis[:].indirect(half_of(con_sb, 1)), ACT.Copy)
-            best_lo = sb("best_lo", [P, HALF], F32)
-            nc.vector.tensor_tensor(best_lo[:], path_lo[:], emis[:, lo], ALU.max)
-            nc.sync.dma_start(out=out[P:V, lo], in_=best_lo[:])
-            path_hi = sb("path_hi", [P, HALF], F32)
-            nc.vector.tensor_tensor(path_hi[:], prev_hi[:], penalty[:, hi], ALU.add)
-            best_hi = sb("best_hi", [P, HALF], F32)
-            nc.vector.tensor_tensor(best_hi[:], path_hi[:], emis[:, hi], ALU.max)
-            nc.sync.dma_start(out=out[P:V, hi], in_=best_hi[:])
+        ds1 = []
+        for g in range(2):
+            ds1.append(sb("ds1%d" % g, [P, HALF], F32))
+            nc.vector.tensor_tensor(ds1[g][:], sc[1][:, half(g)], length[:, half(g)], ALU.subtract)
+        emis = sb("emis", [P, S], F32)
+        for g in range(2):
+            nc.vector.scalar_tensor_tensor(emis[:, half(g)], ds1[g][:], -1.0, ds1[g][:], ALU.mult, ALU.mult)
+        for g in range(2):
+            prev[1, g] = sb("prev1%d" % g, [P, HALF], F32)
+            nc.scalar.activation(prev[1, g][:], emis[:].indirect(list_half(con_sb, g)), ACT.Copy)
 
-        def gather_e_scales():
-            nc.vector.tensor_copy(es[:], es_table[:].indirect(road_sb[:]))
-
-        def gather_e_words():
-            nc.vector.tensor_copy(eq[:], e_table[:].indirect(road_sb[:]))
-
-        for t in range(PACK):
-            window(t)
-            fetch(t, 0)
-            magnitude(t)
-            combine(t, 0)
-        gather_e_words()
-        saturate(0, 0, 2)
-        saturate(0, 2, 4)
-        sc0 = scores(0)
-        for t in range(PACK):
-            step(t, 1)
-        sq0 = squares(sc0, 0)
-        saturate(1, 0, 2)
-        saturate(1, 2, 4)
-        sc1 = scores(1)
-        emit(sq0, 0, 0)
-        emit(sq0, 0, 1)
-        emit1(sc1)
+        for h in range(2):
+            path = []
+            for g in range(2):
+                path.append(sb("path%d%d" % (h, g), [P, HALF], F32))
+                nc.vector.tensor_tensor(path[g][:], prev[h, g][:], toll[:, half(g)], ALU.add)
+            for g in range(2):
+                best = sb("best%d%d" % (h, g), [P, HALF], F32)
+                if h == 0:
+                    nc.vector.scalar_tensor_tensor(best[:], square[:, half(g)], -1.0, path[g][:], ALU.mult, ALU.max)
+                else:
+                    nc.vector.tensor_tensor(best[:], path[g][:], emis[:, half(g)], ALU.max)
+                nc.sync.dma_start(out=out[h * P : (h + 1) * P, half(g)], in_=best[:])

@@ -27,8 +27,8 @@ PENALTY = 0.8
 FLOAT_BIG = 3.0e38
 
 CAST_ON_SCALAR = 64
-COPY_ON_SCALAR = (1,)
-FETCH_ON_VECTOR = ((2, 0), (3, 0))
+COPY_ON_VECTOR = 0
+FETCH_ON_VECTOR = 0
 
 FLOPS = 2 * K * K * S + 2 * K * V * S
 
@@ -91,9 +91,9 @@ def tile_picked_ytrajcl_max_p_kernel(
                     out=table[r:P:QUAD, :].bitcast(I32), in_=scales[0, r : K // QUAD : PACK, :].bitcast(I32)
                 )
 
-        nc.sync.dma_start(out=len_cols[:], in_=len_[0].rearrange("(p c) -> p c", p=P))
-        nc.sync.dma_start(out=unit_sb[:], in_=unit.rearrange("(p t) o -> p (t o)", t=PACK))
         nc.sync.dma_start(offs_sb[:], offs)
+        nc.scalar.dma_start(out=len_cols[:], in_=len_[0].rearrange("(p c) -> p c", p=P))
+        nc.scalar.dma_start(out=unit_sb[:], in_=unit.rearrange("(p t) o -> p (t o)", t=PACK))
         nc.sync.dma_start(out=w_raw[:], in_=w1.rearrange("(p j) c -> p j c", j=PACK))
         load_scales(xs_table, x_scales)
         load_words(x_table, x_words)
@@ -164,15 +164,15 @@ def tile_picked_ytrajcl_max_p_kernel(
         y = []
         for t in range(PACK):
             y.append(sb("y%d" % t, [P, S], F32))
-            if t in COPY_ON_SCALAR:
-                nc.scalar.copy(y[t][:], y_ps[t][:])
-            else:
+            if t == COPY_ON_VECTOR:
                 nc.vector.tensor_copy(y[t][:], y_ps[t][:])
+            else:
+                nc.scalar.copy(y[t][:], y_ps[t][:])
 
         def fetch(t, h):
             yn = sb("yn%d%d" % (t, h), [P, HALF], F32)
             looked_up = y[t][:].indirect(list_half(nxt_sb, h))
-            if (t, h) in FETCH_ON_VECTOR:
+            if h == FETCH_ON_VECTOR:
                 nc.vector.tensor_copy(yn[:], looked_up)
             else:
                 nc.scalar.activation(yn[:], looked_up, ACT.Copy)

from contextlib import ExitStack

import concourse.mybir as mybir

F32 = mybir.dt.float32
BF16 = mybir.dt.bfloat16
I32 = mybir.dt.int32
U32 = mybir.dt.uint32
U16 = mybir.dt.uint16
U8 = mybir.dt.uint8
FP8X4 = mybir.dt.float8_e4m3fn_x4
ALU = mybir.AluOpType
ACT = mybir.ActivationFunctionType

P = 128
QUAD = 32
PACK = 4
K = 512
TABLE = 2048
S = 512
HALF = S // 2
V = 256
GROUP = 16
PSUM_BANKS = 8
SATURATION = 0.8
PENALTY = 0.8
FLOAT_BIG = 3.0e38

CAST_ON_SCALAR = 64
COPY_ON_VECTOR = 0
FETCH_ON_VECTOR = 0

FLOPS = 2 * K * K * S + 2 * K * V * S


def tile_picked_ytrajcl_max_p_kernel(
    tc, x_words, x_scales, w1, e_words, e_scales, unit, len_, offs, nxt, road, con, out
):
    nc = tc.nc
    with ExitStack() as ctx:
        keep = ctx.enter_context(tc.tile_pool(name="keep", bufs=1))
        psum = ctx.enter_context(tc.psum_pool(name="psum", bufs=PSUM_BANKS))

        def sb(name, shape, dtype, tag=None):
            return keep.tile(shape, dtype, name=name, tag=tag or name, align_bytes=64)

        def bank(name, shape):
            return psum.tile(shape, F32, name=name, tag="bank")

        def half(n):
            return slice(n * HALF, (n + 1) * HALF)

        def list_half(entries, n):
            return entries[:, n * (HALF // GROUP) : (n + 1) * (HALF // GROUP)]

        offs_sb = sb("offs_sb", [P, S // GROUP], U16)
        nxt_sb = sb("nxt_sb", [P, S // GROUP], U16)
        road_sb = sb("road_sb", [P, S // GROUP], U16)
        con_sb = sb("con_sb", [P, S // GROUP], U16)
        w_raw = sb("w_raw", [P, PACK, K], F32, tag="w_raw")
        x_table = sb("x_table", [P, TABLE], U32, tag="x_table")
        e_table = sb("e_table", [P, TABLE], U32)
        xs_table = sb("xs_table", [P, TABLE], U8)
        es_table = sb("es_table", [P, TABLE], U8)
        len_cols = sb("len_cols", [P, TABLE // P], F32)
        unit_sb = sb("unit_sb", [P, PACK], F32)
        ident = sb("ident", [P, P], F32)

        nc.gpsimd.memset(xs_table[:].bitcast(I32), 0)
        nc.gpsimd.memset(es_table[:].bitcast(I32), 0)

        ones = sb("ones", [P, P], F32)
        ramp = sb("ramp", [P, P], F32)
        base = sb("base", [P, 1], F32)
        within = sb("within", [P, QUAD], F32)
        row = sb("row", [P, 1], F32)
        nc.vector.memset(ones[:], 1.0)
        for q in range(P // QUAD):
            nc.vector.memset(base[QUAD * q : QUAD * (q + 1), :], float(QUAD * q))
        nc.vector.tensor_tensor_scan(ramp[:], ones[:], ones[:], 0.0, ALU.mult, ALU.add)
        nc.vector.transpose(within[:], ramp[:, 0:QUAD])
        nc.vector.tensor_tensor(row[:], within[:, 0:1], base[:], ALU.add)
        nc.vector.tensor_scalar(ident[:], ramp[:], row[:], None, ALU.is_equal)

        def load_words(table, words):
            nc.sync.dma_start(out=table[:].bitcast(I32), in_=words[0].rearrange("p n t -> p (n t)").bitcast(I32))

        def load_scales(table, scales):
            for r in range(PACK):
                nc.sync.dma_start(
                    out=table[r:P:QUAD, :].bitcast(I32), in_=scales[0, r : K // QUAD : PACK, :].bitcast(I32)
                )

        nc.sync.dma_start(offs_sb[:], offs)
        nc.scalar.dma_start(out=len_cols[:], in_=len_[0].rearrange("(p c) -> p c", p=P))
        nc.scalar.dma_start(out=unit_sb[:], in_=unit.rearrange("(p t) o -> p (t o)", t=PACK))
        nc.sync.dma_start(out=w_raw[:], in_=w1.rearrange("(p j) c -> p j c", j=PACK))
        load_scales(xs_table, x_scales)
        load_words(x_table, x_words)
        nc.sync.dma_start(road_sb[:], road)
        load_scales(es_table, e_scales)
        load_words(e_table, e_words)
        nc.sync.dma_start(nxt_sb[:], nxt)
        nc.sync.dma_start(con_sb[:], con)

        warm = sb("warm", [P, 1], F32)
        warm_out = sb("warm_out", [P, 1], F32)
        nc.vector.memset(warm[:], 1.0)
        nc.scalar.activation(warm_out[:], warm[:], ACT.Abs_reciprocal_sqrt)

        inverse = sb("inverse", [P, PACK], F32)
        per_unit = sb("per_unit", [P, PACK], F32)
        nc.vector.reciprocal(inverse[:], unit_sb[:])
        nc.vector.tensor_scalar(per_unit[:], inverse[:], -FLOAT_BIG, FLOAT_BIG, ALU.max, ALU.min)

        w_bf = sb("w_bf", [P, PACK, P, PACK], BF16)
        w_src = w_raw[:].rearrange("p j (m t) -> p m j t", t=PACK)
        w_dst = w_bf[:].rearrange("p t m j -> p m j t")
        nc.scalar.copy(w_dst[:, :CAST_ON_SCALAR], w_src[:, :CAST_ON_SCALAR])
        nc.vector.tensor_copy(w_dst[:, CAST_ON_SCALAR:], w_src[:, CAST_ON_SCALAR:])
        xs = sb("xs", [P, S], U8)
        nc.vector.tensor_copy(xs[:], xs_table[:].indirect(offs_sb[:]))
        wq = sb("wq", [P, K], U32)
        ws = sb("ws", [P, K], U8)
        nc.vector.quantize_mx(out=wq[:].bitcast(FP8X4), scales=ws[:], in_=w_bf[:].rearrange("p t m j -> p (t m j)"))

        len_table = sb("len_table", [P, TABLE], F32, tag="w_raw")
        len_view = len_table[:].rearrange("p (n c) -> p n c", c=TABLE // P)
        per_bank = S // P
        for first in range(0, TABLE // P, per_bank):
            spread = bank("spread", [P, per_bank, P])
            for c in range(per_bank):
                column = len_cols[:, first + c : first + c + 1]
                nc.tensor.transpose(spread[:, c, :], column.to_broadcast([P, P]), ident[:])
            nc.scalar.copy(len_view[:, :, first : first + per_bank], spread[:].rearrange("p c n -> p n c"))
        length = sb("length", [P, S], F32)
        nc.scalar.activation(length[:], len_table[:].indirect(road_sb[:]), ACT.Copy)

        xq = [sb("xq%d" % h, [P, HALF], U32) for h in range(2)]
        y_ps = [bank("y_ps", [P, S]) for t in range(PACK)]
        for h in range(2):
            nc.vector.tensor_copy(xq[h][:], x_table[:].indirect(list_half(offs_sb, h)))
        for tiles in ((0, 1), (2, 3)):
            for h in range(2):
                for t in tiles:
                    nc.tensor.matmul_mx(
                        out=y_ps[t][:, half(h)],
                        lhsT=wq[:, t * P : (t + 1) * P].bitcast(FP8X4),
                        lhsT_scale=ws[:, t * P : (t + 1) * P],
                        rhs=xq[h][:].bitcast(FP8X4),
                        rhs_scale=xs[:, half(h)],
                        start=True,
                        stop=True,
                    )
        es = sb("es", [P, S], U8, tag="x_table")
        nc.vector.tensor_copy(es[:], es_table[:].indirect(road_sb[:]))

        mag = [sb("mag%d" % t, [P, S], F32) for t in range(PACK)]
        scaled = [sb("scaled%d" % h, [P, PACK, P], F32) for h in range(2)]
        size = [sb("size%d" % h, [P, PACK, P], F32) for h in range(2)]
        root = [sb("root%d" % h, [P, PACK, P], F32) for h in range(2)]
        damp = [sb("damp%d" % h, [P, PACK, P], F32) for h in range(2)]

        y = []
        for t in range(PACK):
            y.append(sb("y%d" % t, [P, S], F32))
            if t == COPY_ON_VECTOR:
                nc.vector.tensor_copy(y[t][:], y_ps[t][:])
            else:
                nc.scalar.copy(y[t][:], y_ps[t][:])

        def fetch(t, h):
            yn = sb("yn%d%d" % (t, h), [P, HALF], F32)
            looked_up = y[t][:].indirect(list_half(nxt_sb, h))
            if h == FETCH_ON_VECTOR:
                nc.vector.tensor_copy(yn[:], looked_up)
            else:
                nc.scalar.activation(yn[:], looked_up, ACT.Copy)
            return yn

        def trajectories(h, yn):
            vel, vy = [], []
            for t in range(PACK):
                vel.append(sb("vel%d%d" % (t, h), [P, HALF], F32))
                nc.vector.tensor_tensor(vel[t][:], yn[t][:], y[t][:, half(h)], ALU.subtract)
            for t in range(PACK):
                vy.append(sb("vy%d%d" % (t, h), [P, HALF], F32))
                nc.vector.scalar_tensor_tensor(
                    vy[t][:], vel[t][:], unit_sb[:, t : t + 1], mag[t][:, half(h)], ALU.mult, ALU.mult
                )
            for t in range(PACK):
                nc.vector.tensor_tensor(scaled[h][:, t, :], vy[t][:, 0::2], vy[t][:, 1::2], ALU.add)

        yn0 = []
        for t in range(PACK):
            yn0.append(fetch(t, 0))
            nc.scalar.activation(mag[t][:], y[t][:], ACT.Abs)
        trajectories(0, yn0)
        trajectories(1, [fetch(t, 1) for t in range(PACK)])

        eq = sb("eq", [P, S], U32, tag="vy31")
        nc.vector.tensor_copy(eq[:], e_table[:].indirect(road_sb[:]))

        for h in range(2):
            for t in range(PACK):
                nc.scalar.activation(size[h][:, t, :], scaled[h][:, t, :], ACT.Abs, scale=per_unit[:, t : t + 1])
            for tiles in (slice(0, 2), slice(2, 4)):
                nc.scalar.activation(
                    root[h][:, tiles, :], size[h][:, tiles, :], ACT.Abs_reciprocal_sqrt, bias=SATURATION
                )
            for tiles in (slice(0, 2), slice(2, 4)):
                nc.scalar.activation(damp[h][:, tiles, :], root[h][:, tiles, :], ACT.Square)

        sc = []
        for h in range(2):
            hid = sb("hid%d" % h, [P, P, PACK], BF16)
            nc.vector.tensor_tensor(
                hid[:].rearrange("p (b i) t -> p b t i", i=4),
                scaled[h][:].rearrange("p t (b i) -> p b t i", i=4),
                damp[h][:].rearrange("p t (b i) -> p b t i", i=4),
                ALU.mult,
            )
            hq = sb("hq%d" % h, [P, P], U32)
            hs = sb("hs%d" % h, [P, P], U8)
            nc.vector.quantize_mx(out=hq[:].bitcast(FP8X4), scales=hs[:], in_=hid[:].rearrange("p v t -> p (v t)"))
            sc.append(bank("sc", [P, S]))
            nc.tensor.matmul_mx(
                out=sc[h][:],
                lhsT=hq[:].bitcast(FP8X4),
                lhsT_scale=hs[:],
                rhs=eq[:].bitcast(FP8X4),
                rhs_scale=es[:],
                start=True,
                stop=True,
            )

        toll = sb("toll", [P, S], F32, tag="root1")
        nc.scalar.activation(toll[:], length[:], ACT.Copy, scale=-PENALTY)

        prev = {}
        ds0 = sb("ds0", [P, S], F32, tag="hid1")
        nc.vector.tensor_tensor(ds0[:], sc[0][:], length[:], ALU.subtract)
        square = sb("square", [P, S], F32)
        nc.scalar.activation(square[:], ds0[:], ACT.Square)
        for g in range(2):
            prev[0, g] = sb("prev0%d" % g, [P, HALF], F32)
            nc.scalar.activation(prev[0, g][:], square[:].indirect(list_half(con_sb, g)), ACT.Copy, scale=-1.0)

        ds1 = []
        for g in range(2):
            ds1.append(sb("ds1%d" % g, [P, HALF], F32))
            nc.vector.tensor_tensor(ds1[g][:], sc[1][:, half(g)], length[:, half(g)], ALU.subtract)
        emis = sb("emis", [P, S], F32)
        for g in range(2):
            nc.vector.scalar_tensor_tensor(emis[:, half(g)], ds1[g][:], -1.0, ds1[g][:], ALU.mult, ALU.mult)
        for g in range(2):
            prev[1, g] = sb("prev1%d" % g, [P, HALF], F32)
            nc.scalar.activation(prev[1, g][:], emis[:].indirect(list_half(con_sb, g)), ACT.Copy)

        for h in range(2):
            path = []
            for g in range(2):
                path.append(sb("path%d%d" % (h, g), [P, HALF], F32))
                nc.vector.tensor_tensor(path[g][:], prev[h, g][:], toll[:, half(g)], ALU.add)
            for g in range(2):
                best = sb("best%d%d" % (h, g), [P, HALF], F32)
                if h == 0:
                    nc.vector.scalar_tensor_tensor(best[:], square[:, half(g)], -1.0, path[g][:], ALU.mult, ALU.max)
                else:
                    nc.vector.tensor_tensor(best[:], path[g][:], emis[:, half(g)], ALU.max)
                nc.sync.dma_start(out=out[h * P : (h + 1) * P, half(g)], in_=best[:])
